import numpy as np
import ml_dtypes

BF16 = ml_dtypes.bfloat16


def bf(x):
    return np.asarray(x, np.float32).astype(BF16)


def f32(x):
    return np.asarray(x, np.float32)


def f64(x):
    return np.asarray(x).astype(np.float64)


def striped(idx):
    return np.tile(idx.reshape(-1, 16).T, (8, 1))


S, K, M, N, B, Q = 512, 128, 128, 384, 2, 192


def setup_inputs():
    return {"base": bf(np.random.standard_normal((B, M, S))), "x": bf(np.random.standard_normal((K, N))), "w": bf(np.random.standard_normal((K, M)) / np.sqrt(K)), "b": f32(0.5 * np.random.standard_normal((M, 1))), "offs": striped(np.random.permutation(S)[:N])}


def reference(base, x, w, b, offs):
    idx = offs[:16].T.reshape(-1)
    z = f64(base).copy()
    for i in range(B):
        z[i][:, idx[i * Q : (i + 1) * Q]] += f64(w).T @ f64(x)[:, i * Q : (i + 1) * Q]
    return np.maximum(z + f64(b), 0.0)

@@ -1,0 +1,59 @@
+import concourse.mybir as mybir
+from concourse.masks import make_identity
+
+BF16, F32, U16 = mybir.dt.bfloat16, mybir.dt.float32, mybir.dt.uint16
+
+P = 128
+S = 512
+B = 2
+Q = 192
+N = B * Q
+QC = Q // 16
+
+FLOPS = 2 * P * P * N
+
+
+def tile_scatter_matmul_kernel(tc, base, x, w, b, offs, out):
+    nc = tc.nc
+    with (
+        tc.tile_pool(name="held", bufs=1) as held,
+        tc.psum_pool(name="windows", bufs=1) as windows,
+    ):
+        offsets = held.tile([P, N // 16], U16, name="offsets")
+        nc.sync.dma_start(offsets[:], offs)
+        base_sb = [held.tile([P, S], BF16, name=f"base{i}") for i in range(B)]
+        nc.sync.dma_start(base_sb[0][:], base[0])
+        nc.scalar.dma_start(base_sb[1][:], base[1])
+        w_sb = held.tile([P, P], BF16, name="w_sb")
+        nc.scalar.dma_start(w_sb[:], w)
+        x_sb = held.tile([P, N], BF16, name="x_sb")
+        nc.sync.dma_start(x_sb[:], x)
+        bias = held.tile([P, 1], F32, name="bias")
+        nc.scalar.dma_start(bias[:], b)
+
+        ident = held.tile([P, P], BF16, name="ident")
+        make_identity(nc, ident[:])
+
+        window = [windows.tile([P, S], F32, name=f"window{i}") for i in range(B)]
+        for i in range(B):
+            nc.tensor.matmul(window[i][:], ident[:], base_sb[i][:], start=True, stop=False)
+
+        for i in range(B):
+            nc.tensor.matmul(
+                window[i][:].indirect(offsets[:, i * QC : (i + 1) * QC]),
+                w_sb[:],
+                x_sb[:, i * Q : (i + 1) * Q],
+                start=False,
+                stop=True,
+            )
+
+        res = [held.tile([P, S], F32, name=f"res{i}") for i in range(B)]
+        nc.scalar.activation(
+            res[0][:], window[0][:], mybir.ActivationFunctionType.Relu, bias=bias[:, 0:1]
+        )
+        nc.vector.tensor_scalar(
+            res[1][:], window[1][:], bias[:, 0:1], 0.0,
+            op0=mybir.AluOpType.add, op1=mybir.AluOpType.max,
+        )
+        nc.scalar.dma_start(out[0], res[0][:])
+        nc.sync.dma_start(out[1], res[1][:])

@@ -8,6 +8,7 @@ S = 512
 B = 2
 Q = 192
 N = B * Q
+H = S // 2
 QC = Q // 16
 
 FLOPS = 2 * P * P * N
@@ -19,17 +20,17 @@ def tile_scatter_matmul_kernel(tc, base, x, w, b, offs, out):
         tc.tile_pool(name="held", bufs=1) as held,
         tc.psum_pool(name="windows", bufs=1) as windows,
     ):
-        offsets = held.tile([P, N // 16], U16, name="offsets")
-        nc.sync.dma_start(offsets[:], offs)
         base_sb = [held.tile([P, S], BF16, name=f"base{i}") for i in range(B)]
         nc.sync.dma_start(base_sb[0][:], base[0])
+        bias = held.tile([P, 1], F32, name="bias")
+        nc.scalar.dma_start(bias[:], b)
         nc.scalar.dma_start(base_sb[1][:], base[1])
+        offsets = held.tile([P, N // 16], U16, name="offsets")
+        nc.sync.dma_start(offsets[:], offs)
         w_sb = held.tile([P, P], BF16, name="w_sb")
         nc.scalar.dma_start(w_sb[:], w)
         x_sb = held.tile([P, N], BF16, name="x_sb")
         nc.sync.dma_start(x_sb[:], x)
-        bias = held.tile([P, 1], F32, name="bias")
-        nc.scalar.dma_start(bias[:], b)
 
         ident = held.tile([P, P], BF16, name="ident")
         make_identity(nc, ident[:])
@@ -48,12 +49,15 @@ def tile_scatter_matmul_kernel(tc, base, x, w, b, offs, out):
             )
 
         res = [held.tile([P, S], F32, name=f"res{i}") for i in range(B)]
-        nc.scalar.activation(
-            res[0][:], window[0][:], mybir.ActivationFunctionType.Relu, bias=bias[:, 0:1]
-        )
-        nc.vector.tensor_scalar(
-            res[1][:], window[1][:], bias[:, 0:1], 0.0,
-            op0=mybir.AluOpType.add, op1=mybir.AluOpType.max,
-        )
-        nc.scalar.dma_start(out[0], res[0][:])
-        nc.sync.dma_start(out[1], res[1][:])
+        for h in range(2):
+            cols = slice(h * H, (h + 1) * H)
+            nc.scalar.activation(
+                res[0][:, cols], window[0][:, cols], mybir.ActivationFunctionType.Relu,
+                bias=bias[:, 0:1],
+            )
+            nc.scalar.dma_start(out[0][:, cols], res[0][:, cols])
+            nc.vector.tensor_scalar(
+                res[1][:, cols], window[1][:, cols], bias[:, 0:1], 0.0,
+                op0=mybir.AluOpType.add, op1=mybir.AluOpType.max,
+            )
+            nc.sync.dma_start(out[1][:, cols], res[1][:, cols])

@@ -9,6 +9,7 @@ B = 2
 Q = 192
 N = B * Q
 H = S // 2
+WARM = 4
 QC = Q // 16
 
 FLOPS = 2 * P * P * N
@@ -34,6 +35,12 @@ def tile_scatter_matmul_kernel(tc, base, x, w, b, offs, out):
 
         ident = held.tile([P, P], BF16, name="ident")
         make_identity(nc, ident[:])
+
+        zeros = held.tile([P, S], BF16, name="zeros")
+        nc.vector.memset(zeros[:], 0.0)
+        idle = windows.tile([P, S], F32, name="idle")
+        for r in range(WARM):
+            nc.tensor.matmul(idle[:], zeros[:, 0:P], zeros[:], start=True, stop=True)
 
         window = [windows.tile([P, S], F32, name=f"window{i}") for i in range(B)]
         for i in range(B):

@@ -9,7 +9,6 @@ B = 2
 Q = 192
 N = B * Q
 H = S // 2
-WARM = 4
 QC = Q // 16
 
 FLOPS = 2 * P * P * N
@@ -23,24 +22,18 @@ def tile_scatter_matmul_kernel(tc, base, x, w, b, offs, out):
     ):
         base_sb = [held.tile([P, S], BF16, name=f"base{i}") for i in range(B)]
         nc.sync.dma_start(base_sb[0][:], base[0])
-        bias = held.tile([P, 1], F32, name="bias")
-        nc.scalar.dma_start(bias[:], b)
         nc.scalar.dma_start(base_sb[1][:], base[1])
         offsets = held.tile([P, N // 16], U16, name="offsets")
         nc.sync.dma_start(offsets[:], offs)
         w_sb = held.tile([P, P], BF16, name="w_sb")
         nc.scalar.dma_start(w_sb[:], w)
+        bias = held.tile([P, 1], F32, name="bias")
+        nc.scalar.dma_start(bias[:], b)
         x_sb = held.tile([P, N], BF16, name="x_sb")
         nc.sync.dma_start(x_sb[:], x)
 
         ident = held.tile([P, P], BF16, name="ident")
         make_identity(nc, ident[:])
-
-        zeros = held.tile([P, S], BF16, name="zeros")
-        nc.vector.memset(zeros[:], 0.0)
-        idle = windows.tile([P, S], F32, name="idle")
-        for r in range(WARM):
-            nc.tensor.matmul(idle[:], zeros[:, 0:P], zeros[:], start=True, stop=True)
 
         window = [windows.tile([P, S], F32, name=f"window{i}") for i in range(B)]
         for i in range(B):
@@ -55,16 +48,13 @@ def tile_scatter_matmul_kernel(tc, base, x, w, b, offs, out):
                 stop=True,
             )
 
-        res = [held.tile([P, S], F32, name=f"res{i}") for i in range(B)]
-        for h in range(2):
-            cols = slice(h * H, (h + 1) * H)
-            nc.scalar.activation(
-                res[0][:, cols], window[0][:, cols], mybir.ActivationFunctionType.Relu,
-                bias=bias[:, 0:1],
-            )
-            nc.scalar.dma_start(out[0][:, cols], res[0][:, cols])
-            nc.vector.tensor_scalar(
-                res[1][:, cols], window[1][:, cols], bias[:, 0:1], 0.0,
-                op0=mybir.AluOpType.add, op1=mybir.AluOpType.max,
-            )
-            nc.sync.dma_start(out[1][:, cols], res[1][:, cols])
+        store_queue = [nc.sync, nc.scalar]
+        for i in range(B):
+            res = held.tile([P, S], F32, name=f"res{i}")
+            for h in range(2):
+                cols = slice(h * H, (h + 1) * H)
+                nc.vector.tensor_scalar(
+                    res[:, cols], window[i][:, cols], bias[:, 0:1], 0.0,
+                    op0=mybir.AluOpType.add, op1=mybir.AluOpType.max,
+                )
+                store_queue[h].dma_start(out[i][:, cols], res[:, cols])

@@ -8,7 +8,6 @@ S = 512
 B = 2
 Q = 192
 N = B * Q
-H = S // 2
 QC = Q // 16
 
 FLOPS = 2 * P * P * N
@@ -22,13 +21,13 @@ def tile_scatter_matmul_kernel(tc, base, x, w, b, offs, out):
     ):
         base_sb = [held.tile([P, S], BF16, name=f"base{i}") for i in range(B)]
         nc.sync.dma_start(base_sb[0][:], base[0])
+        bias = held.tile([P, 1], F32, name="bias")
+        nc.scalar.dma_start(bias[:], b)
         nc.scalar.dma_start(base_sb[1][:], base[1])
         offsets = held.tile([P, N // 16], U16, name="offsets")
         nc.sync.dma_start(offsets[:], offs)
         w_sb = held.tile([P, P], BF16, name="w_sb")
         nc.scalar.dma_start(w_sb[:], w)
-        bias = held.tile([P, 1], F32, name="bias")
-        nc.scalar.dma_start(bias[:], b)
         x_sb = held.tile([P, N], BF16, name="x_sb")
         nc.sync.dma_start(x_sb[:], x)
 
@@ -48,13 +47,13 @@ def tile_scatter_matmul_kernel(tc, base, x, w, b, offs, out):
                 stop=True,
             )
 
-        store_queue = [nc.sync, nc.scalar]
-        for i in range(B):
-            res = held.tile([P, S], F32, name=f"res{i}")
-            for h in range(2):
-                cols = slice(h * H, (h + 1) * H)
-                nc.vector.tensor_scalar(
-                    res[:, cols], window[i][:, cols], bias[:, 0:1], 0.0,
-                    op0=mybir.AluOpType.add, op1=mybir.AluOpType.max,
-                )
-                store_queue[h].dma_start(out[i][:, cols], res[:, cols])
+        res = [held.tile([P, S], F32, name=f"res{i}") for i in range(B)]
+        nc.scalar.activation(
+            res[0][:], window[0][:], mybir.ActivationFunctionType.Relu, bias=bias[:, 0:1]
+        )
+        nc.scalar.dma_start(out[0], res[0][:])
+        nc.vector.tensor_scalar(
+            res[1][:], window[1][:], bias[:, 0:1], 0.0,
+            op0=mybir.AluOpType.add, op1=mybir.AluOpType.max,
+        )
+        nc.sync.dma_start(out[1], res[1][:])

@@ -2,6 +2,7 @@ import concourse.mybir as mybir
 from concourse.masks import make_identity
 
 BF16, F32, U16 = mybir.dt.bfloat16, mybir.dt.float32, mybir.dt.uint16
+RELU = mybir.ActivationFunctionType.Relu
 
 P = 128
 S = 512
@@ -31,6 +32,10 @@ def tile_scatter_matmul_kernel(tc, base, x, w, b, offs, out):
         x_sb = held.tile([P, N], BF16, name="x_sb")
         nc.sync.dma_start(x_sb[:], x)
 
+        early = held.tile([P, 1], F32, name="early")
+        nc.vector.memset(early[:], 0.0)
+        nc.scalar.activation(early[:], early[:], RELU)
+
         ident = held.tile([P, P], BF16, name="ident")
         make_identity(nc, ident[:])
 
@@ -48,9 +53,7 @@ def tile_scatter_matmul_kernel(tc, base, x, w, b, offs, out):
             )
 
         res = [held.tile([P, S], F32, name=f"res{i}") for i in range(B)]
-        nc.scalar.activation(
-            res[0][:], window[0][:], mybir.ActivationFunctionType.Relu, bias=bias[:, 0:1]
-        )
+        nc.scalar.activation(res[0][:], window[0][:], RELU, bias=bias[:, 0:1])
         nc.scalar.dma_start(out[0], res[0][:])
         nc.vector.tensor_scalar(
             res[1][:], window[1][:], bias[:, 0:1], 0.0,

@@ -22,13 +22,13 @@ def tile_scatter_matmul_kernel(tc, base, x, w, b, offs, out):
     ):
         base_sb = [held.tile([P, S], BF16, name=f"base{i}") for i in range(B)]
         nc.sync.dma_start(base_sb[0][:], base[0])
-        bias = held.tile([P, 1], F32, name="bias")
-        nc.scalar.dma_start(bias[:], b)
         nc.scalar.dma_start(base_sb[1][:], base[1])
         offsets = held.tile([P, N // 16], U16, name="offsets")
         nc.sync.dma_start(offsets[:], offs)
         w_sb = held.tile([P, P], BF16, name="w_sb")
         nc.scalar.dma_start(w_sb[:], w)
+        bias = held.tile([P, 1], F32, name="bias")
+        nc.scalar.dma_start(bias[:], b)
         x_sb = held.tile([P, N], BF16, name="x_sb")
         nc.sync.dma_start(x_sb[:], x)
 

@@ -11,6 +11,8 @@ Q = 192
 N = B * Q
 QC = Q // 16
 
+WARM = 2
+
 FLOPS = 2 * P * P * N
 
 
@@ -20,6 +22,12 @@ def tile_scatter_matmul_kernel(tc, base, x, w, b, offs, out):
         tc.tile_pool(name="held", bufs=1) as held,
         tc.psum_pool(name="windows", bufs=1) as windows,
     ):
+        zeros = held.tile([P, S], BF16, name="zeros")
+        nc.vector.memset(zeros[:], 0.0)
+        spare = windows.tile([P, S], F32, name="spare")
+        for turn in range(WARM):
+            nc.tensor.matmul(spare[:], zeros[:, 0:P], zeros[:], start=True, stop=True)
+
         base_sb = [held.tile([P, S], BF16, name=f"base{i}") for i in range(B)]
         nc.sync.dma_start(base_sb[0][:], base[0])
         nc.scalar.dma_start(base_sb[1][:], base[1])

@@ -11,7 +11,7 @@ Q = 192
 N = B * Q
 QC = Q // 16
 
-WARM = 2
+WARM = 3
 
 FLOPS = 2 * P * P * N
 
@@ -22,11 +22,14 @@ def tile_scatter_matmul_kernel(tc, base, x, w, b, offs, out):
         tc.tile_pool(name="held", bufs=1) as held,
         tc.psum_pool(name="windows", bufs=1) as windows,
     ):
-        zeros = held.tile([P, S], BF16, name="zeros")
+        zeros = held.tile([P, P], BF16, name="zeros")
         nc.vector.memset(zeros[:], 0.0)
         spare = windows.tile([P, S], F32, name="spare")
         for turn in range(WARM):
-            nc.tensor.matmul(spare[:], zeros[:, 0:P], zeros[:], start=True, stop=True)
+            nc.tensor.matmul(
+                spare[:], zeros[:], zeros[:].unsqueeze(1).to_broadcast([P, S // P, P]),
+                start=True, stop=True,
+            )
 
         base_sb = [held.tile([P, S], BF16, name=f"base{i}") for i in range(B)]
         nc.sync.dma_start(base_sb[0][:], base[0])

@@ -64,10 +64,10 @@ def tile_scatter_matmul_kernel(tc, base, x, w, b, offs, out):
             )
 
         res = [held.tile([P, S], F32, name=f"res{i}") for i in range(B)]
-        nc.scalar.activation(res[0][:], window[0][:], RELU, bias=bias[:, 0:1])
-        nc.scalar.dma_start(out[0], res[0][:])
         nc.vector.tensor_scalar(
-            res[1][:], window[1][:], bias[:, 0:1], 0.0,
+            res[0][:], window[0][:], bias[:, 0:1], 0.0,
             op0=mybir.AluOpType.add, op1=mybir.AluOpType.max,
         )
-        nc.sync.dma_start(out[1], res[1][:])
+        nc.sync.dma_start(out[0], res[0][:])
+        nc.scalar.activation(res[1][:], window[1][:], RELU, bias=bias[:, 0:1])
+        nc.scalar.dma_start(out[1], res[1][:])

@@ -44,8 +44,7 @@ def tile_scatter_matmul_kernel(tc, base, x, w, b, offs, out):
         nc.sync.dma_start(x_sb[:], x)
 
         early = held.tile([P, 1], F32, name="early")
-        nc.vector.memset(early[:], 0.0)
-        nc.scalar.activation(early[:], early[:], RELU)
+        nc.scalar.activation(early[:], zeros[:, 0:1], RELU)
 
         ident = held.tile([P, P], BF16, name="ident")
         make_identity(nc, ident[:])

import concourse.mybir as mybir
from concourse.masks import make_identity

BF16, F32, U16 = mybir.dt.bfloat16, mybir.dt.float32, mybir.dt.uint16
RELU = mybir.ActivationFunctionType.Relu

P = 128
S = 512
B = 2
Q = 192
N = B * Q
QC = Q // 16

WARM = 3

FLOPS = 2 * P * P * N


def tile_scatter_matmul_kernel(tc, base, x, w, b, offs, out):
    nc = tc.nc
    with (
        tc.tile_pool(name="held", bufs=1) as held,
        tc.psum_pool(name="windows", bufs=1) as windows,
    ):
        zeros = held.tile([P, P], BF16, name="zeros")
        nc.vector.memset(zeros[:], 0.0)
        spare = windows.tile([P, S], F32, name="spare")
        for turn in range(WARM):
            nc.tensor.matmul(
                spare[:], zeros[:], zeros[:].unsqueeze(1).to_broadcast([P, S // P, P]),
                start=True, stop=True,
            )

        base_sb = [held.tile([P, S], BF16, name=f"base{i}") for i in range(B)]
        nc.sync.dma_start(base_sb[0][:], base[0])
        nc.scalar.dma_start(base_sb[1][:], base[1])
        offsets = held.tile([P, N // 16], U16, name="offsets")
        nc.sync.dma_start(offsets[:], offs)
        w_sb = held.tile([P, P], BF16, name="w_sb")
        nc.scalar.dma_start(w_sb[:], w)
        bias = held.tile([P, 1], F32, name="bias")
        nc.scalar.dma_start(bias[:], b)
        x_sb = held.tile([P, N], BF16, name="x_sb")
        nc.sync.dma_start(x_sb[:], x)

        early = held.tile([P, 1], F32, name="early")
        nc.scalar.activation(early[:], zeros[:, 0:1], RELU)

        ident = held.tile([P, P], BF16, name="ident")
        make_identity(nc, ident[:])

        window = [windows.tile([P, S], F32, name=f"window{i}") for i in range(B)]
        for i in range(B):
            nc.tensor.matmul(window[i][:], ident[:], base_sb[i][:], start=True, stop=False)

        for i in range(B):
            nc.tensor.matmul(
                window[i][:].indirect(offsets[:, i * QC : (i + 1) * QC]),
                w_sb[:],
                x_sb[:, i * Q : (i + 1) * Q],
                start=False,
                stop=True,
            )

        res = [held.tile([P, S], F32, name=f"res{i}") for i in range(B)]
        nc.vector.tensor_scalar(
            res[0][:], window[0][:], bias[:, 0:1], 0.0,
            op0=mybir.AluOpType.add, op1=mybir.AluOpType.max,
        )
        nc.sync.dma_start(out[0], res[0][:])
        nc.scalar.activation(res[1][:], window[1][:], RELU, bias=bias[:, 0:1])
        nc.scalar.dma_start(out[1], res[1][:])
